import numpy as np, ml_dtypes
CORES = [83,85,87,115,117,119]
N = 6
F, TK = 64, 64
def setup_inputs(rng):
    return {"x": rng.standard_normal((N, 128, N * TK), dtype=np.float32).astype(ml_dtypes.bfloat16), "w": rng.standard_normal((N, 128, F), dtype=np.float32).astype(ml_dtypes.bfloat16)}
def setup_inputs_big(rng):
    d = setup_inputs(rng)
    for k in ("x", "w"): d[k] = (d[k].astype(np.float32) * 1024.0).astype(d[k].dtype)
    return d
def setup_inputs_small(rng):
    d = setup_inputs(rng)
    for k in ("x", "w"): d[k] = (d[k].astype(np.float32) * (1 / 1024.0)).astype(d[k].dtype)
    return d
def setup_inputs_apart(rng):
    d = setup_inputs(rng)
    f = (10.0 ** rng.permutation(np.linspace(-1.5, 1.5, N))).astype(np.float32).reshape(N, 1, 1)
    for k in ("x", "w"): d[k] = (d[k].astype(np.float32) * f).astype(d[k].dtype)
    return d
def reference(x, w):
    X, W = x.astype(np.float64), w.astype(np.float64)
    y = np.zeros((N, F, N * TK))
    for r in range(N):
        for j in range(N):
            y[r][:, TK * j:TK * j + TK] = W[r].T @ X[j][:, TK * r:TK * r + TK]
    return {"y": y.astype(ml_dtypes.bfloat16 if x.dtype != np.float64 else np.float64)}

@@ -1,0 +1,88 @@
+from concourse.bass import DstId, RemoteDMATransfer
+
+N_RANKS = 6
+TK = 64
+F = 64
+K_FAR = 2
+K_NEAR = 2
+
+SCRATCH = {
+    "xs": ("sbuf", [128, N_RANKS * TK], "bfloat16"),
+    "ws": ("sbuf", [128, F], "bfloat16"),
+    "land": ("sbuf", [128, N_RANKS * TK], "bfloat16"),
+    "ys_home": ("sbuf", [128, N_RANKS * TK], "bfloat16"),
+    "ys_away": ("sbuf", [128, N_RANKS * TK], "bfloat16"),
+    "ps_home": ("psum", [128, 512], "float32"),
+    "ps_away": ("psum", [128, 512], "float32"),
+}
+SEMAPHORES = ["x_in", "w_in", "sent", "arr_home", "arr_away", "mm_home", "mm_away", "cp_home", "cp_away",
+              "st_home", "st_away"]
+
+
+def _span(ranks):
+    lo, hi = min(ranks), max(ranks)
+    assert sorted(ranks) == list(range(lo, hi + 1))
+    return lo * TK, (hi + 1) * TK
+
+
+def _blk(j):
+    return slice(j * TK, (j + 1) * TK)
+
+
+def rank_program(g, core, T, topo):
+    rank = T.rank_of(core)
+    if rank is None:
+        return
+    S = T.sem
+    cores = list(T.cores)
+    others = [j for j in range(len(cores)) if j != rank]
+    near = [j for j in others if topo.chip(cores[j]) == topo.chip(core)]
+    far = [j for j in others if topo.chip(cores[j]) != topo.chip(core)]
+
+    g.sync.dma_start(T.xs[:], T.x[:]).then_inc(S.x_in, 16)
+    g.scalar.dma_start(T.ws[:], T.w[:]).then_inc(S.w_in, 16)
+
+    used = 0
+    transfers = []
+    for j, k, sem in [(j, K_FAR, S.arr_away) for j in far] + [(j, K_NEAR, S.arr_home) for j in near]:
+        dst = cores[j]
+        assert topo.may_write(core, dst)
+        allowed = topo.mask(core, dst) & ~used
+        mine = [e for e in range(allowed.bit_length()) if (allowed >> e) & 1][:k]
+        assert len(mine) == k
+        m = sum(1 << e for e in mine)
+        used |= m
+        rid, pid, _ = topo.addr(dst)
+        transfers.append(RemoteDMATransfer(dst_ids=[DstId(rid=rid, pnc=pid)], dma_engine_mask=m, remote_sem=sem,
+                                           src=T.xs[:, _blk(j)], dst=T.land[:, _blk(rank)]))
+    g.wait_ge(S.x_in, 16)
+    g.remote_dma_fused(transfers, local_sem=S.sent)
+
+    h0, h1 = _span(near + [rank])
+    a0, a1 = _span(far)
+    te, ve = g.tensor, g.vector
+
+    te.wait_ge(S.x_in, 16)
+    te.wait_ge(S.w_in, 16)
+    te.matmul(T.ps_home[0:F, rank * TK - h0:rank * TK - h0 + TK], T.ws[:], T.xs[:, _blk(rank)],
+              start=True, stop=True).then_inc(S.mm_home, 1)
+    te.wait_ge(S.arr_home, K_NEAR * len(near))
+    for j in near:
+        te.matmul(T.ps_home[0:F, j * TK - h0:j * TK - h0 + TK], T.ws[:], T.land[:, _blk(j)],
+                  start=True, stop=True).then_inc(S.mm_home, 1)
+    te.wait_ge(S.arr_away, K_FAR * len(far))
+    te.matmul(T.ps_away[0:F, 0:a1 - a0], T.ws[:], T.land[:, a0:a1], start=True, stop=True).then_inc(S.mm_away, 1)
+
+    ve.wait_ge(S.mm_home, len(near) + 1)
+    ve.tensor_copy(T.ys_home[0:F, 0:h1 - h0], T.ps_home[0:F, 0:h1 - h0]).then_inc(S.cp_home, 1)
+    ve.wait_ge(S.mm_away, 1)
+    ve.tensor_copy(T.ys_away[0:F, 0:a1 - a0], T.ps_away[0:F, 0:a1 - a0]).then_inc(S.cp_away, 1)
+
+    g.sync.wait_ge(S.cp_home, 1)
+    g.sync.dma_start(T.y[:, h0:h1], T.ys_home[0:F, 0:h1 - h0]).then_inc(S.st_home, 16)
+    g.scalar.wait_ge(S.cp_away, 1)
+    g.scalar.dma_start(T.y[:, a0:a1], T.ys_away[0:F, 0:a1 - a0]).then_inc(S.st_away, 16)
+
+    g.wait_ge(S.sent, K_FAR * len(far) + K_NEAR * len(near))
+    g.wait_ge(S.st_home, 16)
+    g.wait_ge(S.st_away, 16)

@@ -3,30 +3,67 @@ from concourse.bass import DstId, RemoteDMATransfer
 N_RANKS = 6
 TK = 64
 F = 64
-K_FAR = 2
-K_NEAR = 2
+GROUPS = ("early", "home", "late")
 
 SCRATCH = {
     "xs": ("sbuf", [128, N_RANKS * TK], "bfloat16"),
     "ws": ("sbuf", [128, F], "bfloat16"),
     "land": ("sbuf", [128, N_RANKS * TK], "bfloat16"),
-    "ys_home": ("sbuf", [128, N_RANKS * TK], "bfloat16"),
-    "ys_away": ("sbuf", [128, N_RANKS * TK], "bfloat16"),
-    "ps_home": ("psum", [128, 512], "float32"),
-    "ps_away": ("psum", [128, 512], "float32"),
+    "ys": ("sbuf", [128, N_RANKS * TK], "bfloat16"),
+    "ps_own": ("psum", [128, 512], "float32"),
 }
-SEMAPHORES = ["x_in", "w_in", "sent", "arr_home", "arr_away", "mm_home", "mm_away", "cp_home", "cp_away",
-              "st_home", "st_away"]
-
-
-def _span(ranks):
-    lo, hi = min(ranks), max(ranks)
-    assert sorted(ranks) == list(range(lo, hi + 1))
-    return lo * TK, (hi + 1) * TK
+SEMAPHORES = ["x_first", "x_rest", "w_in", "sent", "st_sync", "st_scalar", "mm_own", "cp_own"]
+for _n in GROUPS:
+    SCRATCH["ps_" + _n] = ("psum", [128, 512], "float32")
+    SEMAPHORES += ["arr_" + _n, "mm_" + _n, "cp_" + _n]
 
 
 def _blk(j):
     return slice(j * TK, (j + 1) * TK)
+
+
+def _bits(m):
+    return [e for e in range(m.bit_length()) if (m >> e) & 1]
+
+
+def _pow2(n):
+    k = 1
+    while 2 * k <= n:
+        k *= 2
+    return k
+
+
+def _runs(ranks):
+    ranks, out, i = sorted(ranks), [], 0
+    while i < len(ranks):
+        n = 1
+        while i + n < len(ranks) and ranks[i + n] == ranks[i] + n:
+            n += 1
+        out.append(slice(ranks[i] * TK, (ranks[i] + n) * TK))
+        i += n
+    return out
+
+
+def _plan(s, cores, topo):
+    src = cores[s]
+    same = [j for j in range(len(cores)) if topo.chip(cores[j]) == topo.chip(src)]
+    far = [j for j in range(len(cores)) if j not in same]
+    near = [j for j in same if j != s]
+    late = [far[same.index(s) % len(far)]]
+    early = [j for j in far if j not in late]
+    used, part = 0, {}
+    for members, name in ((early, "early"), (near, "home")):
+        free = ~used
+        for j in members:
+            free &= topo.mask(src, cores[j])
+        free = _bits(free)
+        k = _pow2(len(free) // len(members))
+        part[name] = []
+        for i, j in enumerate(members):
+            m = sum(1 << e for e in free[i * k:(i + 1) * k])
+            used |= m
+            part[name].append((j, m, name))
+    return [part["early"], [(late[0], topo.mask(src, cores[late[0]]), "late")] + part["home"]]
 
 
 def rank_program(g, core, T, topo):
@@ -35,54 +72,68 @@ def rank_program(g, core, T, topo):
         return
     S = T.sem
     cores = list(T.cores)
-    others = [j for j in range(len(cores)) if j != rank]
-    near = [j for j in others if topo.chip(cores[j]) == topo.chip(core)]
-    far = [j for j in others if topo.chip(cores[j]) != topo.chip(core)]
+    plan = _plan(rank, cores, topo)
+    queues = (g.sync, g.scalar)
 
-    g.sync.dma_start(T.xs[:], T.x[:]).then_inc(S.x_in, 16)
+    first = [j for j, m, name in plan[0]]
+    rest = [j for j in range(len(cores)) if j not in first]
+    n_first = n_rest = 0
+    for i, cols in enumerate(_runs(first)):
+        queues[i % 2].dma_start(T.xs[:, cols], T.x[:, cols]).then_inc(S.x_first, 16)
+        n_first += 16
+    for i, cols in enumerate(_runs(rest)):
+        queues[i % 2].dma_start(T.xs[:, cols], T.x[:, cols]).then_inc(S.x_rest, 16)
+        n_rest += 16
     g.scalar.dma_start(T.ws[:], T.w[:]).then_inc(S.w_in, 16)
 
-    used = 0
-    transfers = []
-    for j, k, sem in [(j, K_FAR, S.arr_away) for j in far] + [(j, K_NEAR, S.arr_home) for j in near]:
-        dst = cores[j]
-        assert topo.may_write(core, dst)
-        allowed = topo.mask(core, dst) & ~used
-        mine = [e for e in range(allowed.bit_length()) if (allowed >> e) & 1][:k]
-        assert len(mine) == k
-        m = sum(1 << e for e in mine)
-        used |= m
-        rid, pid, _ = topo.addr(dst)
-        transfers.append(RemoteDMATransfer(dst_ids=[DstId(rid=rid, pnc=pid)], dma_engine_mask=m, remote_sem=sem,
-                                           src=T.xs[:, _blk(j)], dst=T.land[:, _blk(rank)]))
-    g.wait_ge(S.x_in, 16)
-    g.remote_dma_fused(transfers, local_sem=S.sent)
+    sent = 0
+    for call, ready, n_ready in zip(plan, (S.x_first, S.x_rest), (n_first, n_rest)):
+        transfers = []
+        for j, m, name in call:
+            assert topo.may_write(core, cores[j])
+            rid, pid, _ = topo.addr(cores[j])
+            transfers.append(RemoteDMATransfer(dst_ids=[DstId(rid=rid, pnc=pid)], dma_engine_mask=m,
+                                               remote_sem=S["arr_" + name], src=T.xs[:, _blk(j)],
+                                               dst=T.land[:, _blk(rank)]))
+            sent += len(_bits(m))
+        g.wait_ge(ready, n_ready)
+        g.remote_dma_fused(transfers, local_sem=S.sent)
 
-    h0, h1 = _span(near + [rank])
-    a0, a1 = _span(far)
+    blocks = {name: [] for name in GROUPS}
+    count = {name: 0 for name in GROUPS}
+    for s in range(len(cores)):
+        if s != rank:
+            for call in _plan(s, cores, topo):
+                for j, m, name in call:
+                    if j == rank:
+                        blocks[name].append(s)
+                        count[name] += len(_bits(m))
+
     te, ve = g.tensor, g.vector
-
-    te.wait_ge(S.x_in, 16)
+    te.wait_ge(S.x_rest, n_rest)
     te.wait_ge(S.w_in, 16)
-    te.matmul(T.ps_home[0:F, rank * TK - h0:rank * TK - h0 + TK], T.ws[:], T.xs[:, _blk(rank)],
-              start=True, stop=True).then_inc(S.mm_home, 1)
-    te.wait_ge(S.arr_home, K_NEAR * len(near))
-    for j in near:
-        te.matmul(T.ps_home[0:F, j * TK - h0:j * TK - h0 + TK], T.ws[:], T.land[:, _blk(j)],
-                  start=True, stop=True).then_inc(S.mm_home, 1)
-    te.wait_ge(S.arr_away, K_FAR * len(far))
-    te.matmul(T.ps_away[0:F, 0:a1 - a0], T.ws[:], T.land[:, a0:a1], start=True, stop=True).then_inc(S.mm_away, 1)
+    te.matmul(T.ps_own[0:F, 0:TK], T.ws[:], T.xs[:, _blk(rank)], start=True, stop=True).then_inc(S.mm_own, 1)
+    ve.wait_ge(S.mm_own, 1)
+    ve.tensor_copy(T.ys[0:F, _blk(rank)], T.ps_own[0:F, 0:TK]).then_inc(S.cp_own, 1)
+    g.sync.wait_ge(S.cp_own, 1)
 
-    ve.wait_ge(S.mm_home, len(near) + 1)
-    ve.tensor_copy(T.ys_home[0:F, 0:h1 - h0], T.ps_home[0:F, 0:h1 - h0]).then_inc(S.cp_home, 1)
-    ve.wait_ge(S.mm_away, 1)
-    ve.tensor_copy(T.ys_away[0:F, 0:a1 - a0], T.ps_away[0:F, 0:a1 - a0]).then_inc(S.cp_away, 1)
+    stores = {"sync": 0, "scalar": 0}
+    for name in GROUPS:
+        ps, bl = T["ps_" + name], blocks[name]
+        te.wait_ge(S["arr_" + name], count[name])
+        for i, j in enumerate(bl):
+            te.matmul(ps[0:F, _blk(i)], T.ws[:], T.land[:, _blk(j)], start=True, stop=True).then_inc(
+                S["mm_" + name], 1)
+        ve.wait_ge(S["mm_" + name], len(bl))
+        for i, j in enumerate(bl):
+            ve.tensor_copy(T.ys[0:F, _blk(j)], ps[0:F, _blk(i)]).then_inc(S["cp_" + name], 1)
+        qn = "scalar" if name == "late" else "sync"
+        q = g.scalar if name == "late" else g.sync
+        q.wait_ge(S["cp_" + name], len(bl))
+        for cols in _runs(bl + [rank] if name == "home" else bl):
+            q.dma_start(T.y[:, cols], T.ys[0:F, cols]).then_inc(S["st_" + qn], 16)
+            stores[qn] += 16
 
-    g.sync.wait_ge(S.cp_home, 1)
-    g.sync.dma_start(T.y[:, h0:h1], T.ys_home[0:F, 0:h1 - h0]).then_inc(S.st_home, 16)
-    g.scalar.wait_ge(S.cp_away, 1)
-    g.scalar.dma_start(T.y[:, a0:a1], T.ys_away[0:F, 0:a1 - a0]).then_inc(S.st_away, 16)
-
-    g.wait_ge(S.sent, K_FAR * len(far) + K_NEAR * len(near))
-    g.wait_ge(S.st_home, 16)
-    g.wait_ge(S.st_away, 16)
+    g.wait_ge(S.sent, sent)
+    g.wait_ge(S.st_sync, stores["sync"])
+    g.wait_ge(S.st_scalar, stores["scalar"])

from concourse.bass import DstId, RemoteDMATransfer

N_RANKS = 6
TK = 64
F = 64
GROUPS = ("early", "home", "late")

SCRATCH = {
    "xs": ("sbuf", [128, N_RANKS * TK], "bfloat16"),
    "ws": ("sbuf", [128, F], "bfloat16"),
    "land": ("sbuf", [128, N_RANKS * TK], "bfloat16"),
    "ys": ("sbuf", [128, N_RANKS * TK], "bfloat16"),
    "ps_own": ("psum", [128, 512], "float32"),
}
SEMAPHORES = ["x_first", "x_rest", "w_in", "sent", "st_sync", "st_scalar", "mm_own", "cp_own"]
for _n in GROUPS:
    SCRATCH["ps_" + _n] = ("psum", [128, 512], "float32")
    SEMAPHORES += ["arr_" + _n, "mm_" + _n, "cp_" + _n]


def _blk(j):
    return slice(j * TK, (j + 1) * TK)


def _bits(m):
    return [e for e in range(m.bit_length()) if (m >> e) & 1]


def _pow2(n):
    k = 1
    while 2 * k <= n:
        k *= 2
    return k


def _runs(ranks):
    ranks, out, i = sorted(ranks), [], 0
    while i < len(ranks):
        n = 1
        while i + n < len(ranks) and ranks[i + n] == ranks[i] + n:
            n += 1
        out.append(slice(ranks[i] * TK, (ranks[i] + n) * TK))
        i += n
    return out


def _plan(s, cores, topo):
    src = cores[s]
    same = [j for j in range(len(cores)) if topo.chip(cores[j]) == topo.chip(src)]
    far = [j for j in range(len(cores)) if j not in same]
    near = [j for j in same if j != s]
    late = [far[same.index(s) % len(far)]]
    early = [j for j in far if j not in late]
    used, part = 0, {}
    for members, name in ((early, "early"), (near, "home")):
        free = ~used
        for j in members:
            free &= topo.mask(src, cores[j])
        free = _bits(free)
        k = _pow2(len(free) // len(members))
        part[name] = []
        for i, j in enumerate(members):
            m = sum(1 << e for e in free[i * k:(i + 1) * k])
            used |= m
            part[name].append((j, m, name))
    return [part["early"], [(late[0], topo.mask(src, cores[late[0]]), "late")] + part["home"]]


def rank_program(g, core, T, topo):
    rank = T.rank_of(core)
    if rank is None:
        return
    S = T.sem
    cores = list(T.cores)
    plan = _plan(rank, cores, topo)
    queues = (g.sync, g.scalar)

    first = [j for j, m, name in plan[0]]
    rest = [j for j in range(len(cores)) if j not in first]
    n_first = n_rest = 0
    for i, cols in enumerate(_runs(first)):
        queues[i % 2].dma_start(T.xs[:, cols], T.x[:, cols]).then_inc(S.x_first, 16)
        n_first += 16
    for i, cols in enumerate(_runs(rest)):
        queues[i % 2].dma_start(T.xs[:, cols], T.x[:, cols]).then_inc(S.x_rest, 16)
        n_rest += 16
    g.scalar.dma_start(T.ws[:], T.w[:]).then_inc(S.w_in, 16)

    sent = 0
    for call, ready, n_ready in zip(plan, (S.x_first, S.x_rest), (n_first, n_rest)):
        transfers = []
        for j, m, name in call:
            assert topo.may_write(core, cores[j])
            rid, pid, _ = topo.addr(cores[j])
            transfers.append(RemoteDMATransfer(dst_ids=[DstId(rid=rid, pnc=pid)], dma_engine_mask=m,
                                               remote_sem=S["arr_" + name], src=T.xs[:, _blk(j)],
                                               dst=T.land[:, _blk(rank)]))
            sent += len(_bits(m))
        g.wait_ge(ready, n_ready)
        g.remote_dma_fused(transfers, local_sem=S.sent)

    blocks = {name: [] for name in GROUPS}
    count = {name: 0 for name in GROUPS}
    for s in range(len(cores)):
        if s != rank:
            for call in _plan(s, cores, topo):
                for j, m, name in call:
                    if j == rank:
                        blocks[name].append(s)
                        count[name] += len(_bits(m))

    te, ve = g.tensor, g.vector
    te.wait_ge(S.x_rest, n_rest)
    te.wait_ge(S.w_in, 16)
    te.matmul(T.ps_own[0:F, 0:TK], T.ws[:], T.xs[:, _blk(rank)], start=True, stop=True).then_inc(S.mm_own, 1)
    ve.wait_ge(S.mm_own, 1)
    ve.tensor_copy(T.ys[0:F, _blk(rank)], T.ps_own[0:F, 0:TK]).then_inc(S.cp_own, 1)
    g.sync.wait_ge(S.cp_own, 1)

    stores = {"sync": 0, "scalar": 0}
    for name in GROUPS:
        ps, bl = T["ps_" + name], blocks[name]
        te.wait_ge(S["arr_" + name], count[name])
        for i, j in enumerate(bl):
            te.matmul(ps[0:F, _blk(i)], T.ws[:], T.land[:, _blk(j)], start=True, stop=True).then_inc(
                S["mm_" + name], 1)
        ve.wait_ge(S["mm_" + name], len(bl))
        for i, j in enumerate(bl):
            ve.tensor_copy(T.ys[0:F, _blk(j)], ps[0:F, _blk(i)]).then_inc(S["cp_" + name], 1)
        qn = "scalar" if name == "late" else "sync"
        q = g.scalar if name == "late" else g.sync
        q.wait_ge(S["cp_" + name], len(bl))
        for cols in _runs(bl + [rank] if name == "home" else bl):
            q.dma_start(T.y[:, cols], T.ys[0:F, cols]).then_inc(S["st_" + qn], 16)
            stores[qn] += 16

    g.wait_ge(S.sent, sent)
    g.wait_ge(S.st_sync, stores["sync"])
    g.wait_ge(S.st_scalar, stores["scalar"])
